import numpy as np, ml_dtypes
CORES = [10,34,74,98]
N = 4
BF = ml_dtypes.bfloat16
def gentries(a):
    return np.ascontiguousarray(a.reshape(8, 16, -1).transpose(0, 2, 1)).reshape(8, -1)
def gtable(e):
    e = np.asarray(e); return np.ascontiguousarray(e.reshape(8, -1, 16).transpose(0, 2, 1)).reshape(128, -1).astype(np.int32)
W, C, RO, K = 4096, 256, 4, 4
M = W - 1
def parts(rng):
    ct = rng.integers(0, W, (N, 8, 16, C)); bk = (16 * rng.random((N, 8, 1, W)) * rng.random((N, 8, 16, W))).astype(np.int64)
    pr = rng.integers(0, 241, (N, 8, 16, C)); pg = rng.integers(0, C, (N, 8, C))
    a = rng.integers(0, W, (N, 8, C)); th = rng.integers(500, 1100, (N, 8, C))
    return ct, bk, pr, pg, a, th
def pack(ct, bk, pr, pg, a, th):
    return {"ct": np.ascontiguousarray(ct.reshape(N, 128, C)).astype(np.int32), "bk": np.ascontiguousarray(bk.reshape(N, 128, W)).astype(np.float32).astype(BF),
            "pr": np.ascontiguousarray(pr.reshape(N, 128, C)).astype(np.int32), "pg": np.stack([gtable(x) for x in pg]), "a0": a.astype(np.int32), "th": th.astype(np.int32)}
def setup_inputs(rng):
    return pack(*parts(rng))
def setup_inputs_ties(rng):
    ct, bk, pr, pg, a, th = parts(rng)
    bk = (rng.random((N, 8, 16, W)) < rng.choice(np.array([0.02, 0.05, 0.1]), (N, 8, 1, 1))).astype(np.int64)
    pr = rng.integers(0, 3, (N, 8, 16, C)); th = rng.integers(0, 20, (N, 8, C))
    pr[:, 1::2] = np.minimum(pr[:, 1::2] + 1, 2)
    bk[:, 0] = rng.integers(1, 5, (N, 16, W)); th[:, 0] = np.add.reduce(pr[:, 0], axis=1) + rng.integers(0, 2, (N, C))
    return pack(ct, bk, pr, pg, a, th)
def setup_inputs_ends(rng):
    ct, bk, pr, pg, a, th = parts(rng); e = np.array([0, 1, W // 2, M - 1, M])
    ct[:, ::2] = e[rng.integers(0, 5, (N, 4, 16, C))]; a[:, ::2] = e[rng.integers(0, 5, (N, 4, C))]
    ct[:, 4, :, ::2] = rng.integers(0, W, (N, 16, C // 2))
    ct[:, 1] = ct[:, 1, :1]
    pg[:, 5] = rng.integers(0, C, (N, 1)); pg[:, 6] = rng.choice(np.array([0, C - 1]), (N, C)); pg[:, 0] = rng.choice(np.array([0, C - 1, 1]), (N, C))
    th = np.where(rng.random(th.shape) < 0.5, th, rng.choice(np.array([0, 4095]), th.shape))
    a[:, 3] = a[:1, 3]; ct[:, 3] = (rng.permutation(W).reshape(16, C) + a[:, 3, None]) & M; pg[:, 3] = np.arange(C); th[:, 3] = 0
    low = int(rng.integers(0, 2)) * (C // 2); dd = low + np.arange(0, C // 2, 2)
    s7 = 16 * (low + 1 + 2 * rng.integers(0, C // 4, (16, C))) + rng.integers(0, 16, (16, C))
    s7[0, dd] = 16 * dd + 1; s7[1, dd] = 16 * dd + 16
    a[:, 7] = a[:1, 7]; ct[:, 7] = (s7 + a[:, 7, None]) & M; pg[:, 7] = np.arange(C); pr[:, 7] = 240
    b7 = bk[:, 7]; b7[:, :, 16 * dd + 1] = rng.integers(9, 16, (N, 16, len(dd))); b7[:, :, 16 * dd + 16] = 0
    v7 = worth(bk[:, 7:8], ((ct - a[:, :, None, :]) & M)[:, 7:8], pr[:, 7:8])[:, 0]
    th[:, 7] = 4095; t7 = th[:, 7]; t7[:, dd] = v7[:, dd] - 16 * rng.integers(0, 2, (N, len(dd)))
    return pack(ct, bk, pr, pg, a, th)
def setup_inputs_full(rng):
    ct, bk, pr, pg, a, th = parts(rng)
    bk[:, ::2] = 15 - rng.integers(0, 4, (N, 4, 16, W)) * (rng.random((N, 4, 16, W)) < 0.1)
    ct[:, 0] &= ~1; a[:, 0] &= ~1
    bk[:, 0, :, 0::2] = 15; bk[:, 0, :, 1::2] = rng.integers(3, 11, (N, 16, W // 2))
    pr[:, ::2] = rng.choice(np.array([240, 240, 239, 238, 232, 225]), (N, 4, 16, C)); pr[:, 0, :, ::2] = 240
    th[:, ::2] = rng.integers(3660, 3820, (N, 4, C)); th[:, 0] = rng.choice(np.array([3800, 3839, 3840, 3841]), (N, C))
    th[:, 0, 0] = 3840; th[:, 0, 2] = 3841
    pr[:, 4, :, 1::2] = 0; th[:, 4, 1::2] = rng.integers(0, 2, (N, C // 2))
    z = W // 4; s1 = rng.integers(0, z, (N, 16, C)); s1[:, 14] = 0; s1[:, 15] = z - 1
    ct[:, 1] = (s1 + a[:, 1, None]) & M; bk[:, 1, :, :z] = 0; bk[:, 1, :, z:] = rng.integers(1, 16, (N, 16, W - z))
    pg[:, 1] = np.argsort(rng.random((N, C)), axis=-1)
    return pack(ct, bk, pr, pg, a, th)
def setup_inputs_crib(rng):
    ct, bk, pr, pg, a, th = parts(rng)
    words = rng.integers(0, W, (8, 16, 4)); plain = np.take_along_axis(words[None], rng.integers(0, 4, (N, 8, 16, C)), 3)
    plain = np.where(rng.random(plain.shape) < 0.25, rng.integers(0, W, plain.shape), plain)
    hs = rng.permutation(W)[:W // 8]; plain[:, 5] = hs[rng.integers(0, W // 8, (N, 16, C))]; plain[:, 5, int(rng.integers(0, K))] = hs[0]
    true = rng.integers(0, W, (N, 8, C)); ct = (plain + true[:, :, None, :]) & M
    a = np.where(rng.random(a.shape) < 0.5, true, a)
    a[:, 5] = true[:, 5]; a[0::2, 5] = (true[0::2, 5] + rng.integers(1, W, true[0::2, 5].shape)) & M
    hot = np.zeros((8, W), bool); hot[np.arange(8)[:, None], words.reshape(8, -1)] = True
    hot[5] = False; hot[5, hs] = True
    bk = np.where(hot[None, :, None, :], rng.integers(7, 16, bk.shape), rng.integers(0, 4, bk.shape))
    th = rng.integers(300, 1700, th.shape); th[:, 7] = 4095
    return pack(ct, bk, pr, pg, a, th)
def setup_inputs_spread(rng):
    ct, bk, pr, pg, a, th = parts(rng)
    ex = rng.choice(np.array([0.2, 1.0, 4.0, 12.0]), (N, 8, 1, W)) * rng.choice(np.array([0.5, 1.0, 2.0]), (N, 8, 16, 1))
    bk = np.minimum((16 * rng.random((N, 8, 16, W)) ** ex).astype(np.int64), 15)
    pr = np.minimum(np.exp2(8 * rng.random((N, 8, 16, C))).astype(np.int64) - 1, 240)
    ct = (ct[:, :, :1] + (np.exp2(12 * rng.random((N, 8, 1, C))) * rng.random((N, 8, 16, C))).astype(np.int64)) & M
    pg = (C * rng.random((N, 8, C)) ** rng.choice(np.array([1.0, 3.0, 8.0]), (N, 8, 1))).astype(np.int64) % C
    th = np.minimum(np.exp2(12 * rng.random((N, 8, C))).astype(np.int64) - 1, 4095)
    return pack(ct, bk, pr, pg, a, th)
def check_inputs(d):
    bad = []
    for k, lo, hi in (("ct", 0, W - 1), ("pr", 0, 240), ("pg", 0, C - 1), ("a0", 0, W - 1), ("th", 0, 4095)):
        if np.min(d[k]) < lo or np.max(d[k]) > hi: bad.append("range of " + k)
    b = np.asarray(d["bk"]).astype(np.float32)
    if np.any(b != np.floor(b)): bad.append("bk holds whole numbers")
    if np.min(b) < 0 or np.max(b) > 15: bad.append("range of bk")
    return bad
def worth(b, s, cap):
    w = np.zeros(cap.shape, np.int32)
    for i in range(16): w = w + np.take_along_axis(b, s[:, :, i:i + 1], 3)
    return np.add.reduce(np.minimum(w, cap), axis=2)
def reference(ct, bk, pr, pg, a0, th):
    x = ct.astype(np.int64).reshape(N, 8, 16, C); cap = pr.astype(np.int32).reshape(N, 8, 16, C)
    b = bk.astype(np.float32).astype(np.int32).reshape(N, 8, 16, W); a = a0.astype(np.int64)
    f = np.stack([gentries(e) for e in pg]).astype(np.int64)
    for t in range(RO):
        s = (x - a[:, :, None, :]) & M
        other = s[[(r + 1 + t % (N - 1)) % N for r in range(N)]]
        z = np.take_along_axis(other, f[:, :, None, :], 3)
        v = worth(b, s, cap); best = a
        for k in range(1, K + 1):
            i = K * t + k - 1
            ak = (x[:, :, i] - z[:, :, i]) & M
            vk = worth(b, (x - ak[:, :, None, :]) & M, cap)
            best = np.where(vk > v, ak, best); v = np.maximum(v, vk)
        a = best
        s = (x - a[:, :, None, :]) & M
        got = np.take_along_axis(b, s.transpose(0, 1, 3, 2).reshape(N, 8, 1, W), 3)
        on = np.repeat(v >= th, 16, axis=2)[:, :, None, :]
        b = np.where(on, b + np.sign(got - b), b)
    return {"ya": a.astype(np.float32), "yv": v.astype(np.float32), "yb": b.reshape(N, 128, W).astype(np.float32).astype(BF)}

import numpy as np
from concourse.mybir import AluOpType, ActivationFunctionType

ALU = AluOpType
AF = ActivationFunctionType
RO = 4
NR = 4
C = 256

SCRATCH = {
    "X32": ("sbuf", [128, 256], "int32"), "AT": ("sbuf", [128, 512], "int32"), "ATH": ("sbuf", [128, 512], "float16"),
    "PG32": ("sbuf", [128, 16], "int32"), "FU": ("sbuf", [128, 16], "uint16"),
    "PR32": ("sbuf", [128, 256], "int32"), "NH": ("sbuf", [128, 256], "bfloat16"), "NH4": ("sbuf", [128, 1024], "bfloat16"),
    "XH": ("sbuf", [128, 256], "float16"), "NXH": ("sbuf", [128, 256], "float16"),
    "S": ("sbuf", [128, 1536], "int32"), "OFFU": ("sbuf", [128, 1024], "uint16"),
    "OZ0": ("sbuf", [128, 256], "uint16"), "OZ1": ("sbuf", [128, 256], "uint16"), "OZ2": ("sbuf", [128, 256], "uint16"),
    "OZ3": ("sbuf", [128, 256], "uint16"), "IDX": ("sbuf", [128, 256], "uint16"),
    "LAND0": ("sbuf", [128, 64], "uint16"), "LAND1": ("sbuf", [128, 256], "uint16"),
    "LAND2": ("sbuf", [128, 256], "uint16"), "LAND3": ("sbuf", [128, 256], "uint16"),
    "ZW": ("sbuf", [128, 256], "float32"), "ZH": ("sbuf", [128, 256], "float16"),
    "G0": ("sbuf", [128, 4096], "bfloat16"), "G14": ("sbuf", [128, 16384], "bfloat16"),
    "R": ("sbuf", [128, 256, 6], "bfloat16"),
    "SC": ("sbuf", [128, 96], "float32"), "D0": ("sbuf", [128, 96], "float32"),
    "C4": ("sbuf", [128, 16], "float32"), "C5": ("sbuf", [128, 16], "float32"), "DC": ("sbuf", [128, 16], "float32"),
    "KI": ("sbuf", [128, 32], "int32"), "KA": ("sbuf", [128, 32], "int32"), "KU": ("sbuf", [128, 32], "uint16"),
    "BK0": ("sbuf", [128, 4096], "bfloat16"), "BK1": ("sbuf", [128, 4096], "bfloat16"),
    "DF": ("sbuf", [128, 4096], "bfloat16"), "CB": ("sbuf", [128, 4096], "bfloat16"),
    "ONES": ("sbuf", [128, 512], "bfloat16"), "NEG": ("sbuf", [128, 128], "bfloat16"), "M2K": ("sbuf", [128, 8], "bfloat16"),
    "M2L": ("sbuf", [128, 8], "bfloat16"),
    "IDN": ("sbuf", [128, 128], "bfloat16"), "NID": ("sbuf", [128, 128], "bfloat16"), "EM": ("sbuf", [128, 128], "bfloat16"),
    "SELM": ("sbuf", [128, 2048], "bfloat16"), "WIDE": ("sbuf", [128, 144], "bfloat16"),
    "P32": ("sbuf", [128, 4], "int32"), "PM": ("sbuf", [128, 4], "int32"), "PMF": ("sbuf", [128, 4], "float32"),
    "PTH": ("sbuf", [128, 4], "float32"),
    "I16": ("sbuf", [128, 256], "int32"), "TF": ("sbuf", [128, 256], "float32"),
    "YI": ("sbuf", [128, 256], "int32"), "YS": ("sbuf", [128, 256], "int32"), "YF": ("sbuf", [128, 256], "float32"),
    "VI": ("sbuf", [128, 16], "int32"), "VH": ("sbuf", [128, 16], "float16"), "VF": ("sbuf", [128, 256], "float32"),
    "ZX": ("sbuf", [128, 144], "bfloat16"), "ZA": ("sbuf", [128, 144], "bfloat16"), "T8": ("sbuf", [128, 8], "int32"),
    "MK": ("sbuf", [128, 8], "float32"), "SELZ": ("sbuf", [128, 512], "bfloat16"), "CI": ("sbuf", [128, 64], "int32"),
    "CU": ("sbuf", [128, 64], "uint16"),
    "PS": ("psum", [128, 4096], "float32"),
}
LOADS = ["ct", "a0", "th", "bk", "pg", "pr"]
SEMAPHORES = (["cv", "ca", "cp", "cg", "st", "sent"] + ["ld_" + n for n in LOADS] + ["arr%d" % t for t in range(RO)]
              + ["dup%d" % t for t in range(RO)])

PARAMS = {
    "chunks": [[128, 128]] * 4, "unit": [[32, 16]] * 4, "unit0": 64, "pieces": [[32, 96, 128]] + [[64, 64, 128]] * 3,
    "learn": ["AAAAAYAY"] * 4, "lbank": [4, 5, 6, 7, 1, 4, 5, 6], "sbank": {5: 2, 7: 0}, "ybank": [7, 2, 0],
    "gamma": 1.56, "f": 1.25, "pe": 0.42, "vfix": 60.0, "afix": 100.0, "hop": 80.0, "rlat": 3500.0, "dlat": 2000.0, "dbw": 250.0,
    "look": 500.0,
    "bias": {"zx": -13.7, "za": -8.2, "em": -18.0, "idn": -18.2, "t8a": -23.0, "t8b": -45.6, "p32": -17.2, "dc0": -2.8, "w_240": 0.7,
             "v_1": -12.1, "v_0": -10.4, "la0": 3.9, "la7": 11.8, "i16": -4.3, "lu6": -13.7, "lu7": -10.8, "st_yv": -18.7, "w_128": 4.8,
             "la3": 25.1, "w_32": 7.8, "ls7": 9.1, "ls5": 3.5, "y0": -13.5, "nid": 0.3, "la6": 8.0, "wide2": 2.5, "yz": 15.3,
             "w_144": -18.4, "lu1": -0.9, "la2": 12.0, "lu0": -11.6, "w_64": -2.9, "w_96": 3.7, "bo": -17.2, "w_160": 15.1,
             "la5": -2.6, "la4": 6.1, "lu3": 12.9, "thr": 11.0, "yc": 12.6, "w0": -10.1, "la1": -5.5, "w_224": 17.9, "y1": -33.9,
             "hsum": -21.1, "w_0": 3.1, "w_208": -7.2, "lr7": 14.8, "lr5": 11.5, "w_176": -7.3, "selm": 2.7, "lu2": 9.5,
             "w_192": -6.6, "y2": 2.8, "wide1": 4.6, "lu4": -5.0, "yv": -7.4, "lu5": 14.6},
}
PLAN = {
    "v": "m2k zx0 wide0 mka d0a pm ones za0 pmf pth mkb na xh dc d0c mk sca scb scc d0b thh nxh neg c5 nh s0a c4a s0b s0c d0d th2 ident "
         "g0_0@0 fu c4 zw0 zw1 zw2 zw3 zh0@0 zh1@0 zh2@0 oa0@0 ob0@0 oa1@0 oc0@0 ob1@0 oa2@0 oc1@0 ob2@0 g14_32@0 oc2@0 g14_96@0 "
         "g14_128@0 g14_192@0 g14_224@0 scan0@0 k4_0@0 k5_0@0 ka0@0 ku0@0 ix0@0 oz0@0 lg2@0 lg1@0 lg0@0 lc1@0 lc2@0 scan1@0 k4_1@0 "
         "k5_1@0 ka1@0 ku1@0 oz1@0 ix1@0 lg3@0 lg6@0 lc0@0 lc3@0 lg4@0 lc6@0 lc4@0 lc5@0 s0n@0 lw4@0 "
         "zw@1 zh1@1 zh2@1 zh0@1 g0_0@1 oa0@1 ob0@1 oa1@1 oc0@1 ob1@1 oa2@1 ob2@1 oc1@1 oc2@1 g14_96@1 g14_32@1 g14_176@1 g14_240@1 "
         "g14_160@1 scan0@1 k4_0@1 k5_0@1 ka0@1 ku0@1 ix0@1 oz0@1 lg1@1 lg0@1 lg2@1 lc1@1 lc0@1 lg3@1 lc2@1 lc3@1 scan1@1 k4_1@1 "
         "k5_1@1 ka1@1 ku1@1 ix1@1 oz1@1 s0n@1 lg4@1 lg6@1 lc4@1 lw3@1 lc6@1 lw7@1 lw6@1 "
         "g0_0@2 zw@2 zh0@2 zh1@2 zh2@2 oa0@2 ob0@2 oa1@2 oc0@2 oa2@2 ob1@2 ob2@2 oc1@2 g14_32@2 oc2@2 g14_96@2 g14_160@2 g14_192@2 "
         "g14_176@2 scan0@2 k5_0@2 k4_0@2 ka0@2 ku0@2 ix0@2 oz0@2 lg0@2 lg1@2 lc0@2 lc1@2 lg2@2 lg3@2 scan1@2 lc2@2 k5_1@2 k4_1@2 "
         "ka1@2 ku1@2 oz1@2 ix1@2 lg4@2 lg6@2 lc7@2 lc6@2 s0n@2 lc4@2 lc3@2 lw7@2 lw3@2 "
         "zw@3 zh1@3 zh0@3 zh2@3 g0_192@3 oa0@3 oa1@3 ob0@3 ob1@3 oc0@3 oa2@3 oc1@3 g14_32@3 ob2@3 oc2@3 g14_96@3 g14_128@3 g14_240@3 "
         "g14_224@3 scan0@3 k5_0@3 k4_0@3 ka0@3 vi0 ku0@3 ix0@3 ys0 lg2@3 lg1@3 lg0@3 lc0@3 lg3@3 lc1@3 lc3@3 lc2@3 scan1@3 k5_1@3 "
         "k4_1@3 ka1@3 vi1 ku1@3 vh ix1@3 lg4@3 lg6@3 lc4@3 ys1 lc7@3 lc6@3 ya1 vf ya2 lw6@3 ya3",
    "a": "ld_a0 ld_pr ld_bk selz0 selz1 selz2 selz3 th1 nh4_0 nh4_2 nh4_3 nh4_1 g0_192@0 g0_64@0 g0_128@0 g14_0@0 g14_64@0 g14_208@0 "
         "g14_160@0 r0@0 g14_144@0 r_0@0 g14_240@0 g14_176@0 r_1@0 lw1@0 lg7@0 lg5@0 lw2@0 lc7@0 lw0@0 lw3@0 lw7@0 lw6@0 lw5@0 "
         "g0_128@1 g0_64@1 g0_192@1 g14_0@1 g14_64@1 r0@1 g14_144@1 g14_192@1 r_0@1 g14_224@1 g14_128@1 g14_208@1 r_1@1 lw1@1 lw0@1 "
         "lw2@1 lg5@1 lg7@1 lc5@1 lc7@1 lw5@1 lw4@1 "
         "g0_128@2 g0_64@2 g0_192@2 g14_0@2 g14_64@2 r0@2 g14_144@2 g14_128@2 r_0@2 g14_208@2 g14_224@2 g14_240@2 r_1@2 lw0@2 lw1@2 "
         "lw2@2 lg7@2 lg5@2 lc5@2 lw5@2 lw4@2 lw6@2 "
         "g0_0@3 g0_128@3 g0_64@3 g14_0@3 g14_64@3 r0@3 g14_176@3 r_0@3 g14_192@3 g14_144@3 g14_160@3 g14_208@3 r_1@3 lw0@3 lw1@3 "
         "lw2@3 lg7@3 lg5@3 lw3@3 lc5@3 lw4@3 lw7@3 lw5@3",
}


def build(T, topo, core, P):
    rank = T.rank_of(core)
    ops = []
    cyc = 0.83 * P["f"]
    gam = P["gamma"]
    masks = {}

    def A(name, *idx):
        if len(idx) == 0:
            idx = (slice(None),)
        shape = SCRATCH[name][1]
        key = (name, repr(idx[1:]))
        if key not in masks:
            m = np.zeros(shape[1:], bool)
            m[idx[1:]] = True
            flat = m.reshape(-1)
            banks = ()
            if name == "PS":
                banks = tuple(b for b in range(8) if flat[512 * b:512 * (b + 1)].any())
            masks[key] = (int.from_bytes(np.packbits(flat).tobytes(), "big"), banks, int(flat.sum()))
        mk = masks[key]
        ap = T[name][idx if len(idx) > 1 else idx[0]]
        return (ap, name, mk[0], mk[1], mk[2])

    al = slice(None)

    def F(name, a=None, b=None, s=None):
        return A(name, al, slice(a, b, s))

    def add(name, kind, engs, cost, instrs, lat=0.0, sem=None, inc=1):
        ops.append({"name": name, "kind": kind, "engs": engs, "cost": cost, "ins": instrs, "lat": lat, "sem": sem, "inc": inc})

    def vcost(n, rate=1.0):
        return P["vfix"] + max(64.0, n * rate) * cyc

    def gcost(n):
        return {"v": 50.0 * P["f"] + n * gam * cyc, "a": 65.0 * P["f"] + n * gam * cyc}

    def dtime(nbytes):
        return P["dlat"] + nbytes / P["dbw"]

    def vop(name, fn, reads, writes, rate=1.0, kind="v"):
        add(name, kind, "v", {"v": vcost(writes[0][4], rate)}, [(fn, reads, writes)])

    def ts(name, out, in0, s1, s2, op0, op1=None, rate=1.0, kind="v"):
        a1 = s1[0] if isinstance(s1, tuple) else s1
        rd = [in0] + ([s1] if isinstance(s1, tuple) else [])
        if op1 is None:
            vop(name, lambda q, e: q.tensor_scalar(out[0], in0[0], a1, None, op0), rd, [out], rate, kind)
        else:
            vop(name, lambda q, e: q.tensor_scalar(out[0], in0[0], a1, s2, op0, op1), rd, [out], rate, kind)

    def tt(name, out, in0, in1, op, rate=2.0, kind="v"):
        vop(name, lambda q, e: q.tensor_tensor(out[0], in0[0], in1[0], op), [in0, in1], [out], rate, kind)

    def cp(name, out, in_, rate=1.0, kind="v"):
        vop(name, lambda q, e: q.tensor_copy(out[0], in_[0]), [in_], [out], rate, kind)

    def ms(name, out, val):
        vop(name, lambda q, e: q.memset(out[0], val), [], [out], 0.5)

    def flex(name, kind, out, in_, vfn, func, scale=1.0, vrate=1.0, col=None):
        def fn(q, e):
            if e == "v":
                return vfn(q)
            if col is None:
                return q.activation(out[0], in_[0], func, scale=scale)
            if func == AF.Relu:
                return q.activation(out[0], in_[0], func, bias=col[0])
            return q.activation(out[0], in_[0], func, scale=col[0])
        n = out[4]
        add(name, kind, "va", {"v": vcost(n, vrate), "a": P["afix"] + max(64.0, n) * cyc}, [(fn, [in_] + ([col] if col else []), [out])])

    def gather(name, kind, out, win, off, engs="va"):
        def fn(q, e):
            src = win[0].indirect(off[0])
            if e == "v":
                return q.tensor_copy(out[0], src)
            return q.activation(out[0], src, AF.Copy)
        add(name, kind, engs, gcost(out[4]), [(fn, [win, off], [out])])

    def mm(name, groups, first=True, final=True):
        ins = []
        cost = 60.0
        for out, terms in groups:
            for j, (l, r) in enumerate(terms):
                def fn(q, e, out=out, l=l, r=r, j=j, n=len(terms)):
                    return q.matmul(out[0], l[0], r[0], first and j == 0, final and j == n - 1)
                ins.append((fn, [l, r], [out]))
                cost += max(64, out[4]) * P["pe"] * P["f"]
        add(name, "p", "p", {"p": cost}, ins)

    def gsel(name, out, in_, pattern, op, base, cm):
        add(name, "g", "g", {"g": 170.0 + 2 * out[4] * cyc},
            [(lambda q, e: q.affine_select(out[0], in_[0], pattern, op, 0.0, base, cm), [in_], [out])])

    def giota(name, out, pattern, cm, small=False, base=0):
        def fn(q, e):
            if small:
                return q.iota(out[0], pattern, base, cm, allow_small_or_imprecise_dtypes=True)
            return q.iota(out[0], pattern, base, cm)
        add(name, "g", "g", {"g": 130.0 + 2 * out[4] * cyc}, [(fn, [], [out])])

    def load(name, eng, out, src, ahead):
        add("ld_" + name, "dma", eng, {eng: 100.0}, [(lambda q, e: q.dma_start(out[0], src), [], [out])], dtime(ahead), "ld_" + name, 16)

    def store(name, dst, src):
        add(name, "dma", "s", {"s": 100.0}, [(lambda q, e: q.dma_start(dst, src[0]), [src], [])], dtime(src[4] * 256), "st", 16)

    def send(t, d0, d1):
        dst = T.cores[(rank - 1 - t % (NR - 1)) % NR]
        rid, pid = topo.addr(dst)[:2]
        mask = topo.mask(core, dst)
        n = len(topo.engines(core, dst))
        src = F("OZ%d" % t if t else "CU", d0, d1)
        land = F("LAND%d" % t, d0, d1)

        def fn(q, e):
            q.remote_dma(land[0], src[0], T.sem["arr%d" % t], T.sem["sent"], pid, rid, mask)
            return None
        add("send%d@%d" % (d0, t), "send", "g", {"g": 1000.0}, [(fn, [src], [land])],
            P["rlat"] - 1000.0 + (d1 - d0) * 256 / 30.0 + (1500.0 if t == 0 else 0.0), "arr%d" % t, n)

    def bank(b, a=0, e=512, s=None):
        return F("PS", 512 * b + a, 512 * b + e, s)

    p8 = slice(0, 8)
    load("ct", "s", A("X32"), T.ct[:], 131072)
    load("a0", "a", A("AT", p8, slice(0, 256)), T.a0[:], 8192)
    load("th", "s", A("AT", p8, slice(256, 512)), T.th[:], 140000)
    load("pr", "a", A("PR32"), T.pr[:], 280000)
    load("bk", "a", A("BK0"), T.bk[:], 1330000)
    load("pg", "s", A("PG32"), T.pg[:], 1330000)
    ms("ones", A("ONES"), 1.0)
    ms("neg", A("NEG"), -1.0)
    ms("m2k", A("M2K"), -2048.0)
    ms("wide0", A("WIDE"), 0.0)
    gsel("idn", A("IDN"), F("ONES", 0, 128), [[-1, 128]], ALU.is_equal, 0, 1)
    gsel("em", A("EM", p8, al), A("ONES", p8, slice(0, 128)), [[-1, 8], [0, 16]], ALU.is_equal, 0, 1)
    giota("p32", F("P32", 0, 1), [[0, 1]], 1)
    ts("pm", F("PM", 0, 1), F("P32", 0, 1), 15, None, ALU.bitwise_and)
    cp("pmf", F("PMF", 0, 1), F("PM", 0, 1))
    ts("pth", F("PTH", 0, 1), F("PMF", 0, 1), -256.0, 2048.0, ALU.mult, ALU.add)
    ts("xh", A("XH"), A("X32"), -2048.0, None, ALU.add, kind="crit")
    ts("na", A("ATH", p8, slice(0, 256)), A("AT", p8, slice(0, 256)), -1.0, 2048.0, ALU.mult, ALU.add, kind="crit")
    ms("zx0", A("ZX"), 0.0)
    ms("za0", A("ZA"), 0.0)
    gsel("zx", F("ZX", 3, 131, 4), F("ONES", 0, 32), [[-16, 8], [-1, 4]], ALU.is_equal, 0, 1)
    gsel("za", A("ZA", p8, slice(3, 131, 4)), A("ONES", p8, slice(0, 32)), [[-1, 8], [0, 4]], ALU.is_equal, 0, 1)
    mm("yc", [(bank(5, 0, 64), [(A("ZA", p8, slice(3 - j, 131 - j)), A("ATH", p8, slice(64 * j, 64 * j + 64))) for j in range(4)] +
               [(F("ZX", 3 - j, 131 - j), F("XH", 64 * j, 64 * j + 64)) for j in range(4)])])
    ts("sca", A("CI"), bank(5, 0, 64), 4096.0, None, ALU.add, kind="crit")
    ts("scb", A("CI"), A("CI"), 4095, None, ALU.bitwise_and, kind="crit")
    cp("scc", A("CU"), A("CI"), kind="crit")
    send(0, 0, 64)
    giota("t8a", F("T8", 0, 4), [[-1, 4]], 1, base=4)
    giota("t8b", F("T8", 4, 8), [[-4, 4]], 1, base=16)
    ts("mka", F("T8", 0, 4), F("T8", 0, 4), 3, None, ALU.bitwise_and)
    ts("mkb", F("T8", 4, 8), F("T8", 4, 8), 12, None, ALU.bitwise_and)
    ts("mk", A("MK"), A("T8"), 0.0, None, ALU.is_equal)
    mm("bo", [(bank(4, 0, 128), [(A("EM", p8, al), A("EM", p8, al))])])
    for j in range(4):
        so, si, sk = F("SELZ", 128 * j, 128 * j + 128), bank(4, 0, 128), F("MK", 4 + j, 5 + j)
        flex("selz%d" % j, "init", so, si, lambda q, so=so, si=si, sk=sk: q.tensor_scalar(so[0], si[0], sk[0], None, ALU.mult),
             AF.Identity, col=sk)
    mm("yz", [(bank(6, 0, 256), [(A("EM", p8, al), A("ATH", p8, slice(0, 256))), (A("IDN"), A("XH"))])])
    ts("s0a", A("YI"), bank(6, 0, 256), 4096.0, None, ALU.add, kind="crit")
    ts("s0b", F("S", 1024, 1280), A("YI"), 4095, None, ALU.bitwise_and, kind="crit")
    cp("s0c", A("OZ0"), F("S", 1024, 1280), kind="crit")

    def selm(t):
        gsel("selm@%d" % t, F("SELM", 512 * t, 512 * (t + 1)), A("ONES"), [[-1, 4], [-16, 8], [0, 16]], ALU.is_equal, -4 * t, 1)
    selm(0)
    ts("nxh", A("NXH"), A("X32"), -1.0, 2048.0, ALU.mult, ALU.add)
    cp("fu", A("FU"), A("PG32"))
    gsel("wide1", A("M2L"), A("M2K"), [[-16, 8]], ALU.is_ge, 0, 1)
    gsel("wide2", F("WIDE", 15, 128, 16), A("M2L"), [[16, 8]], ALU.is_ge, 15, -1)
    giota("dc0", A("DC"), [[16, 16]], 0, True)
    giota("i16", A("I16"), [[16, 256]], 0)
    gsel("nid", A("NID"), A("NEG"), [[-1, 128]], ALU.is_equal, 0, 1)
    ts("dc", A("DC"), A("DC"), F("PMF", 0, 1), None, ALU.add)
    ts("ident", F("S", 1280, 1536), A("I16"), F("PMF", 0, 1), None, ALU.add)
    ts("nh", A("NH"), A("PR32"), -1.0, None, ALU.mult)
    for b in range(4):
        o = F("NH4", b, 1024, 4)
        flex("nh4_%d" % b, "init", o, A("NH"), lambda q, o=o: q.tensor_copy(o[0], T["NH"][:]), AF.Copy, vrate=0.5)
    ts("thh", A("ATH", p8, slice(256, 512)), A("AT", p8, slice(256, 512)), -2048.0, None, ALU.add)
    mm("thr", [(bank(7, 0, 256), [(A("EM", p8, al), A("ATH", p8, slice(256, 512)))])])
    to, ti, tk = A("TF"), bank(7, 0, 256), F("PTH", 0, 1)
    flex("th1", "init", to, ti, lambda q: q.tensor_scalar(to[0], ti[0], tk[0], 0.0, ALU.add, ALU.max), AF.Relu, col=tk)
    ts("th2", A("R", al, al, 5), A("TF"), 256.0, -1.0, ALU.min, ALU.mult)

    def wide(dl):
        return F("WIDE", 15 - dl, 143 - dl)
    mm("hsum", [(bank(3, 0, 16), [(wide(dl), F("NH", dl, 256, 16)) for dl in range(16)])])
    ms("d0a", A("D0"), -1.0)
    ms("d0b", F("D0", 0, 96, 6), -33554432.0)
    ts("d0c", F("D0", 4, 96, 6), A("DC"), 3.0, -1021.0, ALU.mult, ALU.add)
    ts("d0d", F("D0", 5, 96, 6), bank(3, 0, 16), 1792.0, None, ALU.add)
    ts("c5", A("C5"), A("DC"), -768.0, None, ALU.add)
    ts("c4a", A("C4"), A("DC"), 1024.0, None, ALU.add)
    tt("c4", A("C4"), A("C4"), bank(3, 0, 16), ALU.add, 1.0)

    for t in range(RO):
        old = "BK%d" % (t % 2)
        new = "BK%d" % ((t + 1) % 2)
        last = t == RO - 1
        ways = P["learn"][t]
        u0 = P["unit0"]
        for d in range(0, C, u0):
            gather("g0_%d@%d" % (d, t), "g0", F("G0", 16 * d, 16 * (d + u0)), A(old), F("OZ%d" % t, d, d + u0))
        if t == 0:
            for j in range(4):
                ts("zw%d" % j, F("ZW", 64 * j, 64 * j + 64), A("LAND0"), F("MK", j, j + 1), None, ALU.mult, kind="off")
        else:
            cp("zw@%d" % t, A("ZW"), A("LAND%d" % t), kind="off")
        d0 = 0
        for h, n in enumerate(P["pieces"][t]):
            d1 = d0 + n
            zo, zw, fu = F("ZH", d0, d1), A("ZW"), F("FU", d0 // 16, d1 // 16)
            add("zh%d@%d" % (h, t), "off", "v", gcost(n),
                [(lambda q, e, zo=zo, zw=zw, fu=fu: q.tensor_scalar(zo[0], zw[0].indirect(fu[0]), -2048.0, None, ALU.add), [zw, fu], [zo])])
            grp = []
            yb = P["ybank"][h]
            for b in range(4):
                i = 4 * t + 3 - b
                sel = F("SELM", 128 * i, 128 * i + 128)
                grp.append((bank(yb, b, 4 * n, 4), [(A("IDN"), F("XH", d0, d1)), (sel, F("NXH", d0, d1)),
                                                    (sel if t else F("SELZ", 128 * i, 128 * i + 128), F("ZH", d0, d1))]))
            mm("y%d@%d" % (h, t), grp)
            sw = F("S", 4 * d0, 4 * d1)
            ts("oa%d@%d" % (h, t), sw, bank(yb, 0, 4 * n), 6144.0 if t else 12288.0, None, ALU.add, kind="off")
            ts("ob%d@%d" % (h, t), sw, sw, 4095, None, ALU.bitwise_and, kind="off")
            cp("oc%d@%d" % (h, t), F("OFFU", 4 * d0, 4 * d1), sw, kind="off")
            d0 = d1
        bo, bn = A(old), A(new)
        add("dup@%d" % t, "dup", "s", {"s": 100.0}, [(lambda q, e, bo=bo, bn=bn: q.dma_start(bn[0], bo[0]), [bo], [bn])],
            dtime(1048576), "dup%d" % t, 16)
        if not last:
            selm(t + 1)

        def relu(name, out, in_):
            flex(name, "relu", out, in_, lambda q: q.tensor_scalar(out[0], in_[0], -1.0, 0.0, ALU.mult, ALU.max), AF.Relu, scale=-1.0)
        mm("w0@%d" % t, [(bank(3, 256, 512), [(A("IDN"), A("NH"))] + [(A("IDN"), F("G0", i, 4096, 16)) for i in range(16)])])
        relu("r0@%d" % t, A("R", al, al, 4), bank(3, 256, 512))
        d0 = 0
        for ci, n in enumerate(P["chunks"][t]):
            d1 = d0 + n
            wb = (ci + 2) % 3
            u = P["unit"][t][ci]
            for d in range(d0, d1, u):
                gather("g14_%d@%d" % (d, t), "g14", F("G14", 64 * d, 64 * (d + u)), A(old), F("OFFU", 4 * d, 4 * (d + u)))
                mm("w_%d@%d" % (d, t), [(bank(wb, 4 * (d - d0), 4 * (d - d0 + u)),
                                        [(A("IDN"), F("NH4", 4 * d, 4 * (d + u)))] +
                                        [(A("IDN"), F("G14", 64 * d + i, 64 * (d + u), 16)) for i in range(16)])])
            relu("r_%d@%d" % (ci, t), A("R", al, slice(d0, d1), slice(0, 4)), bank(wb, 0, 4 * n))
            h0, h1 = d0 // 16, d1 // 16
            nh = h1 - h0
            kb = bank(3, 6 * h0, 6 * h1)
            mm("v_%d@%d" % (ci, t), [(kb, [(wide(dl), A("R", al, slice(d0 + dl, d1, 16), al)) for dl in range(16)])])
            sc, dz = F("SC", 6 * h0, 6 * h1), F("D0", 6 * h0, 6 * h1)
            vop("scan%d@%d" % (ci, t), lambda q, e, sc=sc, dz=dz, kb=kb: q.tensor_tensor_scan(sc[0], dz[0], kb[0], 0.0, ALU.add, ALU.max),
                [dz, kb], [sc], kind="sel")
            tt("k5_%d@%d" % (ci, t), F("KI", 2 * h0 + nh, 2 * h1), F("SC", 6 * h0 + 5, 6 * h1, 6), F("C5", h0, h1), ALU.add, kind="sel")
            tt("k4_%d@%d" % (ci, t), F("KI", 2 * h0, 2 * h0 + nh), F("SC", 6 * h0 + 4, 6 * h1, 6), F("C4", h0, h1), ALU.add, kind="sel")
            ts("ka%d@%d" % (ci, t), F("KA", 2 * h0, 2 * h1), F("KI", 2 * h0, 2 * h1), 2047, None, ALU.bitwise_and, kind="sel")
            cp("ku%d@%d" % (ci, t), F("KU", 2 * h0, 2 * h1), F("KA", 2 * h0, 2 * h1), kind="sel")
            gather("ix%d@%d" % (ci, t), "sel", F("IDX", d0, d1), A("S"), F("KU", 2 * h0 + nh, 2 * h1), "v")
            if last:
                gather("ys%d" % ci, "out", F("YS", d0, d1), A("S"), F("KU", 2 * h0, 2 * h0 + nh), "v")
                ts("vi%d" % ci, F("VI", h0, h1), F("KI", 2 * h0, 2 * h0 + nh), 11, None, ALU.arith_shift_right, kind="out")
            else:
                gather("oz%d@%d" % (ci, t), "sel", F("OZ%d" % (t + 1), d0, d1), A("S"), F("KU", 2 * h0, 2 * h0 + nh), "v")
                send(t + 1, d0, d1)
            d0 = d1
        if last:
            tt("ya1", A("YI"), A("X32"), A("YS"), ALU.subtract, kind="out")
            ts("ya2", A("YI"), A("YI"), 4095, None, ALU.bitwise_and, kind="out")
            cp("ya3", A("YF"), A("YI"), kind="out")
            store("st_ya", T.ya[:], A("YF", slice(0, 128, 16), al))
            ts("vh", A("VH"), A("VI"), -2048.0, None, ALU.add, kind="out")
            mm("yv", [(A("PS", p8, slice(1792 + dl, 2048, 16)), [(F("SELM", 128 * dl, 128 * dl + 128, 16), A("VH"))]) for dl in range(16)])
            vo, vi = A("VF", p8, al), A("PS", p8, slice(1792, 2048))
            ts("vf", vo, vi, 2048.0, None, ALU.add, kind="out")
            store("st_yv", T.yv[:], vo)
        else:
            cp("s0n@%d" % t, F("S", 1024, 1280), A("OZ%d" % (t + 1)), kind="late")
        u = C // len(ways)
        for j, way in enumerate(ways):
            c0, c1 = 16 * u * j, 16 * u * (j + 1)
            ix, ub, df, cb, wn = F("IDX", u * j, u * (j + 1)), F(old, c0, c1), F("DF", c0, c1), F("CB", c0, c1), A(old)
            nb = F(new, c0, c1)
            pb = bank(P["lbank"][j], 0, c1 - c0)
            if way == "A":
                add("lg%d@%d" % (j, t), "lg", "v", gcost(c1 - c0),
                    [(lambda q, e, df=df, wn=wn, ix=ix, nb=nb: q.tensor_tensor(df[0], wn[0].indirect(ix[0]), nb[0], ALU.subtract),
                      [wn, ix, nb], [df])])
                ts("lc%d@%d" % (j, t), cb, df, 1.0, -1.0, ALU.min, ALU.max, rate=0.5, kind="lc")
            else:
                gather("lg%d@%d" % (j, t), "lga", df, wn, ix, "a")
                sb = bank(P["sbank"][j], 0, c1 - c0)
                mm("lr%d@%d" % (j, t), [(sb, [(A("NID"), ub)])], final=False)
                mm("ls%d@%d" % (j, t), [(sb, [(A("IDN"), df)])], first=False)
                flex("lc%d@%d" % (j, t), "lcp", cb, sb,
                     lambda q, cb=cb, sb=sb: q.tensor_scalar(cb[0], sb[0], 1.0, -1.0, ALU.min, ALU.max), AF.Sign)
            mm("lu%d@%d" % (j, t), [(pb, [(A("IDN"), ub)])], final=False)
            mm("la%d@%d" % (j, t), [(pb, [(A("IDN"), cb)])], first=False)
            flex("lw%d@%d" % (j, t), "lw", nb, pb, lambda q, nb=nb, pb=pb: q.tensor_copy(nb[0], pb[0]), AF.Copy)
            if last:
                store("st_yb%d" % j, T.yb[:, c0:c1], nb)
    return ops


def hazards(ops):
    acc = {}
    bank_other = {}
    bank_pe = {}
    for k, op in enumerate(ops):
        pe = op["engs"] == "p"
        ideps = []
        new = []
        for fn, reads, writes in op["ins"]:
            d = set()
            for regs, wr in ((reads, False), (writes, True)):
                for r in regs:
                    for (j, m, w) in acc.get(r[1], []):
                        if (w or wr) and (m & r[2]):
                            d.add(j)
                    for b in r[3]:
                        if b in bank_other:
                            d.add(bank_other[b])
                        if not pe:
                            d.update(bank_pe.get(b, []))
                    new.append((r, wr))
            ideps.append(d)
        merged = {}
        for r, wr in new:
            merged[(r[1], wr)] = merged.get((r[1], wr), 0) | r[2]
            for b in r[3]:
                if pe:
                    bank_pe.setdefault(b, []).append(k)
                else:
                    bank_other[b] = k
                    bank_pe[b] = []
        for (name, wr), m in merged.items():
            lst = acc.get(name, [])
            if wr:
                lst = [x for x in lst if x[1] & ~m]
            acc[name] = lst + [(k, m, wr)]
        op["ideps"] = ideps
        op["deps"] = set().union(*ideps)


def schedule(ops, P, plan):
    n = len(ops)
    hop = P["hop"]
    index = {op["name"]: k for k, op in enumerate(ops)}
    seq = {e: [index[x] for x in plan[e].split()] for e in "va"}
    succ = [[] for _ in range(n)]
    rank = []
    for k, op in enumerate(ops):
        for j in op["deps"]:
            succ[j].append(k)
        nm = op["name"].split("@")
        rank.append((0 if op["kind"] == "send" else 2, (int(nm[1]) if len(nm) > 1 else 0) * 30 + P["bias"].get(nm[0], 0), k))
    left = [len(op["deps"]) for op in ops]
    rt = [0.0] * n
    free = {e: 0.0 for e in "vapgs"}
    pos = {"v": 0, "a": 0}
    ready = {e: [k for k in range(n) if left[k] == 0 and ops[k]["engs"] == e] for e in "pgs"}
    order = []
    while len(order) < n:
        best = None
        for e in "va":
            if pos[e] < len(seq[e]) and left[seq[e][pos[e]]] == 0:
                k = seq[e][pos[e]]
                t0 = max(free[e], rt[k])
                if best is None or t0 < best[0]:
                    best = (t0, e, k)
        for e in "pgs":
            if ready[e]:
                t0 = max(free[e], min(rt[k] for k in ready[e]))
                if best is None or t0 < best[0]:
                    look = P["look"] if e == "g" else 0.0
                    best = (t0, e, min((k for k in ready[e] if rt[k] <= t0 + look), key=lambda j: rank[j]))
        t0, e, k = best
        op = ops[k]
        start = max(t0, rt[k])
        free[e] = start + op["cost"][e]
        fin = free[e] + op["lat"]
        if e in pos:
            pos[e] += 1
        else:
            ready[e].remove(k)
        op["eng"] = e
        op["t"] = (start, fin)
        order.append(k)
        for j in succ[k]:
            rt[j] = max(rt[j], fin + hop)
            left[j] -= 1
            if left[j] == 0 and ops[j]["engs"] in ready:
                ready[ops[j]["engs"]].append(j)
    return order


def emit(g, T, ops, order):
    queues = {"v": g.vector, "a": g.scalar, "p": g.tensor, "g": g, "s": g.sync}
    counter = {"v": "cv", "a": "ca", "p": "cp", "g": "cg"}
    total = {}
    for k in order:
        op = ops[k]
        s = op["sem"] or counter[op["eng"]]
        total[s] = total.get(s, 0) + op["inc"]
        op["sig"] = (s, total[s])
    for op in ops:
        if op["kind"] == "send":
            op["sig"] = (op["sem"], total[op["sem"]])
    clock = {e: {} for e in queues}
    waited = {}
    sent = 0
    for k in order:
        op = ops[k]
        e = op["eng"]
        q = queues[e]
        res = None
        for (fn, reads, writes), deps in zip(op["ins"], op["ideps"]):
            need = {}
            for j in deps:
                s, v = ops[j]["sig"]
                if clock[e].get(s, 0) < v and need.get(s, (0, None))[0] < v:
                    need[s] = (v, j)
            for s, (v, j) in sorted(need.items(), key=lambda x: -ops[x[1][1]]["t"][1]):
                if clock[e].get(s, 0) >= v:
                    continue
                q.wait_ge(T.sem[s], v)
                waited[s] = max(waited.get(s, 0), v)
                clock[e][s] = v
                for s2, v2 in ops[j]["clock"].items():
                    if clock[e].get(s2, 0) < v2:
                        clock[e][s2] = v2
            res = fn(q, e)
        if op["kind"] == "send":
            op["clock"] = {}
            sent += op["inc"]
        else:
            op["clock"] = dict(clock[e])
            res.then_inc(T.sem[op["sig"][0]], op["inc"])
    g.wait_ge(T.sem["sent"], sent)
    for s in sorted(total):
        if waited.get(s, 0) < total[s]:
            g.sync.wait_ge(T.sem[s], total[s])


def rank_program(g, core, T, topo):
    if T.rank_of(core) is None:
        return
    ops = build(T, topo, core, PARAMS)
    hazards(ops)
    emit(g, T, ops, schedule(ops, PARAMS, PLAN))
